import numpy as np, ml_dtypes
CORES = [8,11,14,16,19,22,24,27,30]
N = 9
NH, QP = 3, 256
def setup_inputs(rng):
    return {"q": rng.standard_normal((N, 128, NH * QP), dtype=np.float32).astype(ml_dtypes.bfloat16), "k": rng.standard_normal((N, 128, NH * 128), dtype=np.float32).astype(ml_dtypes.bfloat16), "v": rng.standard_normal((N, 128, NH * 128), dtype=np.float32).astype(ml_dtypes.bfloat16)}
def setup_inputs_big(rng):
    d = setup_inputs(rng)
    for k in ("q", "k", "v"): d[k] = (d[k].astype(np.float32) * 1024.0).astype(d[k].dtype)
    return d
def setup_inputs_small(rng):
    d = setup_inputs(rng)
    for k in ("q", "k", "v"): d[k] = (d[k].astype(np.float32) * (1 / 1024.0)).astype(d[k].dtype)
    return d
def setup_inputs_apart(rng):
    d = setup_inputs(rng)
    f = (10.0 ** rng.permutation(np.linspace(-1.5, 1.5, N))).astype(np.float32).reshape(N, 1, 1)
    for k in ("q", "k", "v"): d[k] = (d[k].astype(np.float32) * f).astype(d[k].dtype)
    return d
def reference(q, k, v):
    Q, K, V = q.astype(np.float64), k.astype(np.float64), v.astype(np.float64)
    y = np.zeros((N, 128, NH * QP))
    for r in range(N):
        for h in range(NH):
            for j in range(N):
                S = np.maximum(K[j][:, 128 * h:128 * h + 128].T @ Q[r][:, QP * h:QP * h + QP], 0.0)
                y[r][:, QP * h:QP * h + QP] += V[j][:, 128 * h:128 * h + 128].T @ S
    return {"y": y.astype(ml_dtypes.bfloat16 if q.dtype != np.float64 else np.float64)}

@@ -1,0 +1,292 @@
+from concourse.bass import DstId, RemoteDMATransfer
+from concourse.mybir import AluOpType
+
+NSIM = 32
+NH, QP, KP = 3, 256, 128
+NR = 9
+NB = 5
+AHEAD = 2
+
+SCRATCH = {
+    "stage": ("sbuf", [128, NH, QP + 2 * KP], "bfloat16"),
+    "kvl": ("sbuf", [128, NR * NH, 2 * KP], "bfloat16"),
+    "ql": ("sbuf", [128, NH, QP], "bfloat16"),
+    "zero": ("sbuf", [128, QP], "bfloat16"),
+    "relu": ("sbuf", [128, 18, QP], "bfloat16"),
+    "obuf": ("sbuf", [128, NH, QP], "bfloat16"),
+    "part": ("sbuf", [128, NH, QP], "bfloat16"),
+    "oland": ("sbuf", [128, NH, QP], "bfloat16"),
+}
+for _i in range(NH):
+    SCRATCH["acc%d" % _i] = ("psum", [128, 512], "float32")
+for _i in range(NB):
+    SCRATCH["s%d" % _i] = ("psum", [128, 512], "float32")
+
+SEMAPHORES = (["lk%d" % h for h in range(NH)] + ["lq%d" % h for h in range(NH)]
+              + ["kv%d_%d" % (j, h) for j in range(NR) for h in range(NH)]
+              + ["q%d" % p for p in range(NH)] + ["o%d" % h for h in range(NH)]
+              + ["zs", "sm", "rl", "om", "ev", "pt", "ls", "st"])
+
+
+def _bits(mask):
+    return [e for e in range(32) if (mask >> e) & 1]
+
+
+def _plan(cores, topo):
+    rank = {c: i for i, c in enumerate(cores)}
+    chips = sorted({topo.chip(c) for c in cores})
+    on = {ch: [c for c in cores if topo.chip(c) == ch] for ch in chips}
+    helper, ports = {}, {}
+    for ch in chips:
+        free = [c for c in range(NSIM) if topo.chip(c) == ch and c not in rank]
+        reach = {c: all(topo.may_write(c, d) for d in cores) for c in free}
+        ports[ch] = [c for c in free if reach[c]]
+        for h, own in enumerate(on[ch]):
+            free.sort(key=lambda c: (topo.die(c) != topo.die(own), not reach[c], c))
+            helper[ch, h] = free.pop(0)
+    calls = {c: [] for c in range(NSIM)}
+    arr, fwd, blocked, relayed_to = {}, {}, {}, set()
+
+    def add(core, waits, trs):
+        for t in trs:
+            for d in t["dsts"]:
+                arr[d, t["sem"]] = arr.get((d, t["sem"]), 0) + len(t["engs"])
+        calls[core].append((waits, trs))
+
+    def kv(j, h, dsts, engs, own):
+        return {"src": ("skv", h) if own else ("kvl", NH * j + h), "dst": ("kvl", NH * j + h), "dsts": dsts,
+                "sem": "kv%d_%d" % (j, h), "engs": engs}
+
+    for j, s in enumerate(cores):
+        ch = topo.chip(s)
+        p = on[ch].index(s)
+        far = [c for c in chips if c != ch]
+        eall = _bits(topo.mask(s, helper[ch, 0]))
+        eoff = _bits(topo.mask(s, on[far[0]][0]))
+        eon = [e for e in eall if e not in eoff]
+        hs = [(p + i) % NH for i in range(NH)]
+        direct = {h: [on[c][h] for c in far if topo.may_write(s, on[c][h])] for h in hs}
+        barred = {h: [on[c][h] for c in far if not topo.may_write(s, on[c][h])] for h in hs}
+        blocked[s] = any(barred[h] for h in hs)
+
+        def qtr(h, engs):
+            return {"src": ("sq", h), "dst": ("ql", p), "dsts": [helper[ch, h]] + ([on[ch][h]] if h != p else []),
+                    "sem": "q%d" % p, "engs": engs}
+
+        if not blocked[s]:
+            half = len(eon) // 2
+            for h in hs:
+                w = len(eoff) // len(direct[h])
+                trs = [kv(j, h, [d], eoff[i * w:(i + 1) * w], True) for i, d in enumerate(direct[h])]
+                trs.append(kv(j, h, [helper[ch, h]], eon[:half], True))
+                trs.append(qtr(h, eon[half:]))
+                add(s, [("lk%d" % h, 32), ("lq%d" % h, 16)], trs)
+            continue
+        load = {c: 0 for c in ports[ch]}
+        extra = {h: [] for h in hs}
+        for h in hs:
+            if barred[h] and helper[ch, h] in load:
+                fwd.setdefault(helper[ch, h], []).append((j, h, list(barred[h])))
+                load[helper[ch, h]] += len(barred[h])
+        for h in hs:
+            if helper[ch, h] in load:
+                continue
+            for d in barred[h]:
+                x = min(load, key=lambda c: (load[c], c))
+                load[x] += 1
+                fwd.setdefault(x, []).append((j, h, [d]))
+                if x not in extra[h]:
+                    extra[h].append(x)
+        for h in hs:
+            for d in barred[h]:
+                relayed_to.add((j, d))
+        q4 = len(eoff) // 2
+        big = max(hs, key=lambda h: len(extra[h]))
+        rest = [h for h in hs if h != big]
+        add(s, [("lk%d" % h, 32) for h in hs],
+            [kv(j, big, [helper[ch, big]] + extra[big], eon, True)]
+            + [kv(j, h, [helper[ch, h]] + extra[h], eoff[i * q4:(i + 1) * q4], True) for i, h in enumerate(rest)])
+        dh = [h for h in hs if direct[h]]
+        if dh:
+            cut = [eoff[:q4], eoff[q4:q4 + q4 // 2], eoff[q4 + q4 // 2:]]
+            add(s, [], [kv(j, h, direct[h], cut[i], True) for i, h in enumerate(dh)])
+        add(s, [("lq%d" % h, 16) for h in hs],
+            [qtr(p, eoff[:q4]), qtr(hs[1], eoff[q4:]), qtr(hs[2], eon)])
+    for x, lst in fwd.items():
+        for j, h, dsts in lst:
+            eoff = _bits(topo.mask(x, dsts[0]))
+            w = len(eoff) // len(dsts)
+            add(x, [("kv%d_%d" % (j, h), None)],
+                [kv(j, h, [d], eoff[i * w:(i + 1) * w], False) for i, d in enumerate(dsts)])
+    return {"rank": rank, "chips": chips, "on": on, "helper": helper, "calls": calls, "arr": arr,
+            "blocked": blocked, "relayed": relayed_to}
+
+
+def _mask(engs):
+    m = 0
+    for e in engs:
+        m |= 1 << e
+    return m
+
+
+def rank_program(g, core, T, topo):
+    cores = list(T.cores)
+    P = _plan(cores, topo)
+    on, helper, arr, blocked = P["on"], P["helper"], P["arr"], P["blocked"]
+    ch = topo.chip(core)
+    if ch not in on:
+        return
+    is_rank = core in P["rank"]
+    heads = [h for h in range(NH) if helper[ch, h] == core]
+    if not is_rank and not heads:
+        return
+    sem = T.sem
+    sent = [0]
+
+    def ap(spec):
+        kind, i = spec
+        if kind == "skv":
+            return T.stage[:, i, QP:QP + 2 * KP]
+        if kind == "sq":
+            return T.stage[:, i, 0:QP]
+        if kind == "kvl":
+            return T.kvl[:, i, :]
+        return T.ql[:, i, :]
+
+    def dst_id(d):
+        rid, pid, _ = topo.addr(d)
+        return DstId(rid=rid, pnc=pid)
+
+    def write(out, in_, d, name):
+        rid, pid, _ = topo.addr(d)
+        m = topo.mask(core, d)
+        g.remote_dma(out, in_, sem[name], sem.ls, pid, rid, m)
+        sent[0] += len(_bits(m))
+
+    if is_rank:
+        p = on[ch].index(core)
+        head = p
+        hs = [(p + i) % NH for i in range(NH)]
+        if blocked[core]:
+            items = [(w, h) for h in hs for w in "kv"] + [("q", h) for h in hs]
+        else:
+            items = [(w, h) for h in hs for w in "kvq"]
+        for i, (w, h) in enumerate(items):
+            qu = g.sync if i % 2 == 0 else g.scalar
+            if w == "k":
+                qu.dma_start(T.stage[:, h, QP:QP + KP], T.k[:, KP * h:KP * h + KP]).then_inc(sem["lk%d" % h], 16)
+            elif w == "v":
+                qu.dma_start(T.stage[:, h, QP + KP:QP + 2 * KP],
+                             T.v[:, KP * h:KP * h + KP]).then_inc(sem["lk%d" % h], 16)
+            else:
+                qu.dma_start(T.stage[:, h, 0:QP], T.q[:, QP * h:QP * h + QP]).then_inc(sem["lq%d" % h], 16)
+    else:
+        p = None
+        head = heads[0]
+
+    for waits, trs in P["calls"][core]:
+        for name, n in waits:
+            g.wait_ge(sem[name], arr[core, name] if n is None else n)
+        g.remote_dma_fused(
+            [RemoteDMATransfer(dst_ids=[dst_id(d) for d in t["dsts"]], dma_engine_mask=_mask(t["engs"]),
+                               remote_sem=sem[t["sem"]], srcs=[ap(t["src"])], dsts=[ap(t["dst"]) for _ in t["dsts"]],
+                               alu_op=0) for t in trs], local_sem=sem.ls)
+        sent[0] += sum(len(t["engs"]) for t in trs)
+
+    loc = on[ch]
+
+    def t_kv(c):
+        return 0.5 if blocked[c] else (head - loc.index(c)) % NH
+
+    def t_q(c):
+        return 1.5 if blocked[c] else (head - loc.index(c)) % NH
+
+    units = []
+    if is_rank:
+        def when(c):
+            j = P["rank"][c]
+            a, b = topo.chip(c), ch
+            two = 0.0 if (topo.mates(a, b) or topo.same_plane(a, b)) else 0.25
+            if (j, core) in P["relayed"]:
+                return 3.0 + two
+            if blocked[c]:
+                return 1.5 + two
+            return (head - on[a].index(c)) % NH + two
+        rem = sorted([c for c in cores if topo.chip(c) != ch], key=lambda c: (when(c), c))
+        peers = sorted([r for r in range(NH) if r != p], key=lambda r: t_q(loc[r]))
+        for i, c in enumerate(rem):
+            order = peers + [p] if i == len(rem) - 1 else [p] + peers
+            units += [(P["rank"][c], r) for r in order]
+    else:
+        pairs = [(c, r) for c in loc for r in range(NH)]
+        pairs.sort(key=lambda cr: (max(t_kv(cr[0]), t_q(loc[cr[1]])), cr[1], cr[0]))
+        units = [(P["rank"][c], r) for c, r in pairs]
+    U = len(units)
+    first = {r: min(i for i, u in enumerate(units) if u[1] == r) for r in range(NH)}
+    last = {r: max(i for i, u in enumerate(units) if u[1] == r) for r in range(NH)}
+    fin = sorted(range(NH), key=lambda r: last[r])
+
+    te, ve = g.tensor, g.vector
+    seen = set()
+
+    def twait(name, n):
+        if name not in seen:
+            seen.add(name)
+            te.wait_ge(sem[name], n)
+
+    for i in range(U + AHEAD):
+        if i >= AHEAD:
+            u = i - AHEAD
+            j, r = units[u]
+            te.wait_ge(sem.rl, u + 1)
+            mm = te.matmul(T["acc%d" % r][:, 0:QP], T.kvl[:, NH * j + head, KP:2 * KP], T.relu[:, u, :],
+                           u == first[r], u == last[r])
+            if u == last[r]:
+                mm.then_inc(sem.om, 1)
+        if i < U:
+            j, r = units[i]
+            name = "kv%d_%d" % (j, head)
+            twait(name, arr[core, name])
+            if is_rank and r == p:
+                twait("lq%d" % head, 16)
+                qa = T.stage[:, head, 0:QP]
+            else:
+                twait("q%d" % r, arr[core, "q%d" % r])
+                qa = T.ql[:, r, :]
+            te.matmul(T["s%d" % (i % NB)][:, 0:QP], T.kvl[:, NH * j + head, 0:KP], qa, True, True).then_inc(sem.sm, 1)
+
+    ve.memset(T.zero[:, :], 0.0).then_inc(sem.zs, 1)
+    ve.wait_ge(sem.zs, 1)
+    for u in range(U):
+        ve.wait_ge(sem.sm, u + 1)
+        ve.tensor_tensor(T.relu[:, u, :], T["s%d" % (u % NB)][:, 0:QP], T.zero[:, :], AluOpType.max).then_inc(sem.rl, 1)
+    if is_rank:
+        ve.wait_ge(sem.pt, arr_part(topo, helper[ch, head], core))
+    for n, r in enumerate(fin):
+        ve.wait_ge(sem.om, n + 1)
+        if is_rank:
+            ve.tensor_tensor(T.obuf[:, r, :], T["acc%d" % r][:, 0:QP], T.part[:, r, :],
+                             AluOpType.add).then_inc(sem.ev, 1)
+        else:
+            ve.tensor_copy(T.obuf[:, r, :], T["acc%d" % r][:, 0:QP]).then_inc(sem.ev, 1)
+
+    if not is_rank:
+        g.wait_ge(sem.ev, NH)
+        write(T.part[:, :, :], T.obuf[:, :, :], loc[head], "pt")
+        g.wait_ge(sem.ls, sent[0])
+        return
+    for n, r in enumerate(fin):
+        if r != p:
+            g.wait_ge(sem.ev, n + 1)
+            write(T.oland[:, head, :], T.obuf[:, r, :], loc[r], "o%d" % head)
+    g.sync.wait_ge(sem.ev, NH)
+    g.sync.dma_start(T.y[:, QP * p:QP * p + QP], T.obuf[:, p, :]).then_inc(sem.st, 16)
+    for qu, h in zip((g.sync, g.scalar), [h for h in range(NH) if h != p]):
+        qu.wait_ge(sem["o%d" % h], len(_bits(topo.mask(loc[h], core))))
+        qu.dma_start(T.y[:, QP * h:QP * h + QP], T.oland[:, h, :]).then_inc(sem.st, 16)
+    g.wait_ge(sem.ls, sent[0])
+    g.wait_ge(sem.st, 16 * NH)
+
+
+def arr_part(topo, src, dst):
+    return len(_bits(topo.mask(src, dst)))

@@ -4,122 +4,40 @@ from concourse.mybir import AluOpType
 NSIM = 32
 NH, QP, KP = 3, 256, 128
 NR = 9
-NB = 5
+KV = 2 * KP
+NACC = 6
+NB = 2
 AHEAD = 2
 
 SCRATCH = {
-    "stage": ("sbuf", [128, NH, QP + 2 * KP], "bfloat16"),
-    "kvl": ("sbuf", [128, NR * NH, 2 * KP], "bfloat16"),
-    "ql": ("sbuf", [128, NH, QP], "bfloat16"),
+    "skv": ("sbuf", [128, NH * KV], "bfloat16"),
+    "sq": ("sbuf", [128, NH * QP], "bfloat16"),
+    "kvl": ("sbuf", [128, NR, NH * KV], "bfloat16"),
+    "ql": ("sbuf", [128, NH, NH * QP], "bfloat16"),
+    "rbuf": ("sbuf", [128, 2, NH * KP], "bfloat16"),
     "zero": ("sbuf", [128, QP], "bfloat16"),
+    "ones": ("sbuf", [128, KP], "bfloat16"),
+    "ident": ("sbuf", [128, KP], "bfloat16"),
     "relu": ("sbuf", [128, 18, QP], "bfloat16"),
-    "obuf": ("sbuf", [128, NH, QP], "bfloat16"),
-    "part": ("sbuf", [128, NH, QP], "bfloat16"),
-    "oland": ("sbuf", [128, NH, QP], "bfloat16"),
+    "obuf": ("sbuf", [128, NH, 2, QP], "bfloat16"),
+    "part": ("sbuf", [128, 10, QP], "bfloat16"),
+    "ybuf": ("sbuf", [128, NH, QP], "bfloat16"),
 }
-for _i in range(NH):
+for _i in range(NACC):
     SCRATCH["acc%d" % _i] = ("psum", [128, 512], "float32")
 for _i in range(NB):
     SCRATCH["s%d" % _i] = ("psum", [128, 512], "float32")
 
 SEMAPHORES = (["lk%d" % h for h in range(NH)] + ["lq%d" % h for h in range(NH)]
               + ["kv%d_%d" % (j, h) for j in range(NR) for h in range(NH)]
-              + ["q%d" % p for p in range(NH)] + ["o%d" % h for h in range(NH)]
-              + ["zs", "sm", "rl", "om", "ev", "pt", "ls", "st"])
+              + ["kw%d" % j for j in range(NR)]
+              + ["q%d_%d" % (r, h) for r in range(NH) for h in range(NH)]
+              + ["rh0", "rh1"] + ["pp%d" % n for n in range(10)]
+              + ["zs", "idn", "sm", "rl", "om", "ev", "ls", "st"])
 
 
 def _bits(mask):
     return [e for e in range(32) if (mask >> e) & 1]
-
-
-def _plan(cores, topo):
-    rank = {c: i for i, c in enumerate(cores)}
-    chips = sorted({topo.chip(c) for c in cores})
-    on = {ch: [c for c in cores if topo.chip(c) == ch] for ch in chips}
-    helper, ports = {}, {}
-    for ch in chips:
-        free = [c for c in range(NSIM) if topo.chip(c) == ch and c not in rank]
-        reach = {c: all(topo.may_write(c, d) for d in cores) for c in free}
-        ports[ch] = [c for c in free if reach[c]]
-        for h, own in enumerate(on[ch]):
-            free.sort(key=lambda c: (topo.die(c) != topo.die(own), not reach[c], c))
-            helper[ch, h] = free.pop(0)
-    calls = {c: [] for c in range(NSIM)}
-    arr, fwd, blocked, relayed_to = {}, {}, {}, set()
-
-    def add(core, waits, trs):
-        for t in trs:
-            for d in t["dsts"]:
-                arr[d, t["sem"]] = arr.get((d, t["sem"]), 0) + len(t["engs"])
-        calls[core].append((waits, trs))
-
-    def kv(j, h, dsts, engs, own):
-        return {"src": ("skv", h) if own else ("kvl", NH * j + h), "dst": ("kvl", NH * j + h), "dsts": dsts,
-                "sem": "kv%d_%d" % (j, h), "engs": engs}
-
-    for j, s in enumerate(cores):
-        ch = topo.chip(s)
-        p = on[ch].index(s)
-        far = [c for c in chips if c != ch]
-        eall = _bits(topo.mask(s, helper[ch, 0]))
-        eoff = _bits(topo.mask(s, on[far[0]][0]))
-        eon = [e for e in eall if e not in eoff]
-        hs = [(p + i) % NH for i in range(NH)]
-        direct = {h: [on[c][h] for c in far if topo.may_write(s, on[c][h])] for h in hs}
-        barred = {h: [on[c][h] for c in far if not topo.may_write(s, on[c][h])] for h in hs}
-        blocked[s] = any(barred[h] for h in hs)
-
-        def qtr(h, engs):
-            return {"src": ("sq", h), "dst": ("ql", p), "dsts": [helper[ch, h]] + ([on[ch][h]] if h != p else []),
-                    "sem": "q%d" % p, "engs": engs}
-
-        if not blocked[s]:
-            half = len(eon) // 2
-            for h in hs:
-                w = len(eoff) // len(direct[h])
-                trs = [kv(j, h, [d], eoff[i * w:(i + 1) * w], True) for i, d in enumerate(direct[h])]
-                trs.append(kv(j, h, [helper[ch, h]], eon[:half], True))
-                trs.append(qtr(h, eon[half:]))
-                add(s, [("lk%d" % h, 32), ("lq%d" % h, 16)], trs)
-            continue
-        load = {c: 0 for c in ports[ch]}
-        extra = {h: [] for h in hs}
-        for h in hs:
-            if barred[h] and helper[ch, h] in load:
-                fwd.setdefault(helper[ch, h], []).append((j, h, list(barred[h])))
-                load[helper[ch, h]] += len(barred[h])
-        for h in hs:
-            if helper[ch, h] in load:
-                continue
-            for d in barred[h]:
-                x = min(load, key=lambda c: (load[c], c))
-                load[x] += 1
-                fwd.setdefault(x, []).append((j, h, [d]))
-                if x not in extra[h]:
-                    extra[h].append(x)
-        for h in hs:
-            for d in barred[h]:
-                relayed_to.add((j, d))
-        q4 = len(eoff) // 2
-        big = max(hs, key=lambda h: len(extra[h]))
-        rest = [h for h in hs if h != big]
-        add(s, [("lk%d" % h, 32) for h in hs],
-            [kv(j, big, [helper[ch, big]] + extra[big], eon, True)]
-            + [kv(j, h, [helper[ch, h]] + extra[h], eoff[i * q4:(i + 1) * q4], True) for i, h in enumerate(rest)])
-        dh = [h for h in hs if direct[h]]
-        if dh:
-            cut = [eoff[:q4], eoff[q4:q4 + q4 // 2], eoff[q4 + q4 // 2:]]
-            add(s, [], [kv(j, h, direct[h], cut[i], True) for i, h in enumerate(dh)])
-        add(s, [("lq%d" % h, 16) for h in hs],
-            [qtr(p, eoff[:q4]), qtr(hs[1], eoff[q4:]), qtr(hs[2], eon)])
-    for x, lst in fwd.items():
-        for j, h, dsts in lst:
-            eoff = _bits(topo.mask(x, dsts[0]))
-            w = len(eoff) // len(dsts)
-            add(x, [("kv%d_%d" % (j, h), None)],
-                [kv(j, h, [d], eoff[i * w:(i + 1) * w], False) for i, d in enumerate(dsts)])
-    return {"rank": rank, "chips": chips, "on": on, "helper": helper, "calls": calls, "arr": arr,
-            "blocked": blocked, "relayed": relayed_to}
 
 
 def _mask(engs):
@@ -129,60 +47,214 @@ def _mask(engs):
     return m
 
 
+def _split(engs, n):
+    w = 1
+    while w * 2 * n <= len(engs):
+        w *= 2
+    return [engs[i * w:(i + 1) * w] for i in range(n)]
+
+
+def _plan(cores, topo):
+    rank = {c: i for i, c in enumerate(cores)}
+    allchips = sorted({topo.chip(c) for c in range(NSIM)})
+    chips = [ch for ch in allchips if any(topo.chip(c) == ch for c in cores)]
+    on = {ch: [c for c in cores if topo.chip(c) == ch] for ch in chips}
+    free = {ch: [c for c in range(NSIM) if topo.chip(c) == ch and c not in rank] for ch in allchips}
+
+    def hops(a, b):
+        return 0 if a == b else (1 if topo.mates(a, b) or topo.same_plane(a, b) else 2)
+
+    late = {ch: [s for s in cores if topo.chip(s) != ch and not all(topo.may_write(s, d) for d in on[ch])]
+            for ch in chips}
+    blocked = {s: any(s in late[ch] for ch in chips) for s in cores}
+
+    def when(s, ch, h):
+        a = topo.chip(s)
+        return (h - on[a].index(s)) % NH + (2.0 if blocked[s] else 0.0) + 0.25 * hops(a, ch)
+
+    work = {c: [] for ch in chips for c in free[ch]}
+    keys, dest, pairs = {}, {}, {}
+    for ch in chips:
+        loc = on[ch]
+        nl, nf = len(loc), len(free[ch])
+        pcs = []
+        for h in range(NH):
+            lst = [(when(s, ch, h), s, h) for s in cores if topo.chip(s) != ch and s not in late[ch]]
+            pcs += sorted(lst, key=lambda x: (x[0], x[1]))
+        for n, (_, s, h) in enumerate(pcs):
+            w = free[ch][min(nf - 1, int((n + 0.5) * nf / len(pcs)))]
+            dest[ch, s, h] = w
+            work[w] += [(rank[s], h, r) for r in range(nl)]
+        pairs[ch] = []
+        for w in free[ch]:
+            hq = []
+            for _, h, _r in work[w]:
+                if h not in hq:
+                    hq.append(h)
+            if len(hq) == 2:
+                grp = [[u for u in work[w] if u[1] == h] for h in hq[::-1]]
+            else:
+                grp = [[u for u in work[w] if u[:2] == work[w][0][:2]], [u for u in work[w] if u[:2] != work[w][0][:2]]]
+            grp = [x for x in grp if x]
+            pairs[ch] += [(w, x[0][1], i) for i, x in enumerate(grp)]
+            work[w] = [u + (i * NH + u[2],) for i, x in enumerate(grp) for u in x]
+        for p, c in enumerate(loc):
+            keys[c] = ([c] + [loc[(p + i) % nl] for i in range(1, nl)]
+                       + sorted(late[ch], key=lambda s: (hops(topo.chip(s), ch), s)))
+
+    relay = {}
+    for s in cores:
+        ch = topo.chip(s)
+        for c in chips:
+            if s not in late[c]:
+                continue
+            mid = []
+            if hops(ch, c) == 2:
+                mid = [x for x in allchips if x not in on and hops(ch, x) == 1 and hops(x, c) == 1]
+            two = []
+            for xc in mid + [ch]:
+                rel = [x for x in free[xc] if topo.may_write(s, x) and all(topo.may_write(x, d) for d in on[c])]
+                byd = {}
+                for x in rel:
+                    byd.setdefault(topo.die(x), x)
+                two = sorted(byd.values())[:2] if len(byd) >= 2 else rel[:2]
+                if len(two) == 2:
+                    break
+            relay[s, c] = two
+    weng = {w: _bits(topo.mask(w, on[[c for c in chips if c != ch][0]][0])) for ch in chips for w in free[ch]}
+
+    calls = {c: [] for c in range(NSIM)}
+    arr, fwd, nslot = {}, {}, {}
+
+    def add(core, waits, trs):
+        for t in trs:
+            for d in t["dsts"]:
+                arr[d, t["sem"]] = arr.get((d, t["sem"]), 0) + len(t["engs"])
+        calls[core].append((waits, trs))
+
+    for j, s in enumerate(cores):
+        ch = topo.chip(s)
+        p = on[ch].index(s)
+        far = [c for c in chips if c != ch]
+        eall = _bits(topo.mask(s, free[ch][0]))
+        eoff = _bits(topo.mask(s, on[far[0]][0]))
+        eon = [e for e in eall if e not in eoff]
+        hs = [(p + i) % NH for i in range(NH)]
+
+        def deal(offs, ons):
+            for t, e in zip(offs, _split(eoff, max(1, len(offs)))):
+                t["engs"] = e
+            for t, e in zip(ons, _split(eon if offs else eall, max(1, len(ons)))):
+                t["engs"] = e
+            return offs + ons
+
+        offs, ons = [], []
+        half = NH * KP
+        for c in far:
+            if s not in late[c]:
+                continue
+            for i, x in enumerate(relay[s, c]):
+                slot = nslot.get(x, 0)
+                nslot[x] = slot + 1
+                t = {"src": ("skv", i * half, (i + 1) * half), "dst": ("rb", slot), "dsts": [x], "sem": "rh%d" % slot}
+                (ons if topo.chip(x) == ch else offs).append(t)
+                fwd.setdefault(x, []).append((j, i * half, (i + 1) * half, slot, list(on[c])))
+        whole = [{"src": ("skv", 0, NH * KV), "dst": ("kvl", j, 0, NH * KV), "dsts": [c for c in on[ch] if c != s],
+                  "sem": "kw%d" % j}]
+        if blocked[s]:
+            add(s, [("lk%d" % h, 32) for h in hs], deal(offs, ons))
+            add(s, [], deal([], whole))
+        for h in hs:
+            lo = KV * h
+            offs = [{"src": ("skv", lo, lo + KV), "dst": ("kvl", j, lo, lo + KV), "dsts": [dest[c, s, h]],
+                     "sem": "kv%d_%d" % (j, h)} for c in far if s not in late[c]]
+            qd = [w for w in free[ch] if any(u[1] == h for u in work[w])]
+            ons = [{"src": ("sq", h), "dst": ("ql", p, h), "dsts": qd, "sem": "q%d_%d" % (p, h)}]
+            add(s, [("lk%d" % h, 32), ("lq%d" % h, 16)], deal(offs, ons))
+        if not blocked[s]:
+            add(s, [], deal([], whole))
+    for x, lst in fwd.items():
+        for j, lo, hi, slot, dsts in lst:
+            add(x, [("rh%d" % slot, None)],
+                [{"src": ("rb", slot), "dst": ("kvl", j, lo, hi), "dsts": dsts, "sem": "kw%d" % j,
+                  "engs": _bits(topo.mask(x, dsts[0]))}])
+    return {"rank": rank, "on": on, "free": free, "calls": calls, "arr": arr, "blocked": blocked,
+            "work": work, "keys": keys, "pairs": pairs, "weng": weng}
+
+
 def rank_program(g, core, T, topo):
     cores = list(T.cores)
     P = _plan(cores, topo)
-    on, helper, arr, blocked = P["on"], P["helper"], P["arr"], P["blocked"]
+    on, arr, work = P["on"], P["arr"], P["work"]
     ch = topo.chip(core)
-    if ch not in on:
-        return
     is_rank = core in P["rank"]
-    heads = [h for h in range(NH) if helper[ch, h] == core]
-    if not is_rank and not heads:
+    mine = work.get(core, [])
+    if not is_rank and not mine and not P["calls"][core]:
         return
     sem = T.sem
     sent = [0]
+    te, ve = g.tensor, g.vector
 
     def ap(spec):
-        kind, i = spec
+        kind = spec[0]
         if kind == "skv":
-            return T.stage[:, i, QP:QP + 2 * KP]
+            return T.skv[:, spec[1]:spec[2]]
         if kind == "sq":
-            return T.stage[:, i, 0:QP]
+            return T.sq[:, QP * spec[1]:QP * spec[1] + QP]
         if kind == "kvl":
-            return T.kvl[:, i, :]
-        return T.ql[:, i, :]
+            return T.kvl[:, spec[1], spec[2]:spec[3]]
+        if kind == "ql":
+            return T.ql[:, spec[1], QP * spec[2]:QP * spec[2] + QP]
+        return T.rbuf[:, spec[1], :]
 
     def dst_id(d):
         rid, pid, _ = topo.addr(d)
         return DstId(rid=rid, pnc=pid)
 
-    def write(out, in_, d, name):
-        rid, pid, _ = topo.addr(d)
-        m = topo.mask(core, d)
-        g.remote_dma(out, in_, sem[name], sem.ls, pid, rid, m)
-        sent[0] += len(_bits(m))
+    idops, vecp = [], {}
+    units = []
+    if is_rank:
+        loc = on[ch]
+        pl = P["pairs"][ch]
+        p = loc.index(core)
+        hs = [(p + i) % NH for i in range(NH)]
+        for c in P["keys"][core]:
+            units += [(P["rank"][c], h, p, h) for h in (hs if c == core else range(NH))]
+        for h in range(NH):
+            ph = sorted((i, n) for n, (w, hh, i) in enumerate(pl) if hh == h)
+            if ph:
+                vecp[h] = ph[-1][1]
+            idops += [(i, n, h, (i, n) == ph[-2]) for i, n in ph[:-1]]
+        idops = [x[1:] for x in sorted(idops)]
+    elif mine:
+        loc = on[ch]
+        pl = P["pairs"][ch]
+        units = list(mine)
 
     if is_rank:
-        p = on[ch].index(core)
-        head = p
-        hs = [(p + i) % NH for i in range(NH)]
-        if blocked[core]:
+        if P["blocked"][core]:
             items = [(w, h) for h in hs for w in "kv"] + [("q", h) for h in hs]
         else:
             items = [(w, h) for h in hs for w in "kvq"]
         for i, (w, h) in enumerate(items):
             qu = g.sync if i % 2 == 0 else g.scalar
             if w == "k":
-                qu.dma_start(T.stage[:, h, QP:QP + KP], T.k[:, KP * h:KP * h + KP]).then_inc(sem["lk%d" % h], 16)
+                qu.dma_start(T.skv[:, KV * h:KV * h + KP], T.k[:, KP * h:KP * h + KP]).then_inc(sem["lk%d" % h], 16)
             elif w == "v":
-                qu.dma_start(T.stage[:, h, QP + KP:QP + 2 * KP],
+                qu.dma_start(T.skv[:, KV * h + KP:KV * h + KV],
                              T.v[:, KP * h:KP * h + KP]).then_inc(sem["lk%d" % h], 16)
             else:
-                qu.dma_start(T.stage[:, h, 0:QP], T.q[:, QP * h:QP * h + QP]).then_inc(sem["lq%d" % h], 16)
-    else:
-        p = None
-        head = heads[0]
+                qu.dma_start(T.sq[:, QP * h:QP * h + QP], T.q[:, QP * h:QP * h + QP]).then_inc(sem["lq%d" % h], 16)
+
+    nz = 0
+    if units:
+        ve.memset(T.zero[:, :], 0.0).then_inc(sem.zs, 1)
+        nz = 1
+        if idops:
+            ve.memset(T.ones[:, :], 1.0).then_inc(sem.zs, 1)
+            nz = 2
+            g.wait_ge(sem.zs, nz)
+            g.affine_select(T.ident[:, :], T.ones[:, :], [[-1, KP]], AluOpType.is_equal, 0.0, 0, 1).then_inc(sem.idn, 1)
 
     for waits, trs in P["calls"][core]:
         for name, n in waits:
@@ -192,41 +264,27 @@ def rank_program(g, core, T, topo):
                                remote_sem=sem[t["sem"]], srcs=[ap(t["src"])], dsts=[ap(t["dst"]) for _ in t["dsts"]],
                                alu_op=0) for t in trs], local_sem=sem.ls)
         sent[0] += sum(len(t["engs"]) for t in trs)
+    if not units:
+        g.wait_ge(sem.ls, sent[0])
+        return
 
-    loc = on[ch]
-
-    def t_kv(c):
-        return 0.5 if blocked[c] else (head - loc.index(c)) % NH
-
-    def t_q(c):
-        return 1.5 if blocked[c] else (head - loc.index(c)) % NH
-
-    units = []
-    if is_rank:
-        def when(c):
-            j = P["rank"][c]
-            a, b = topo.chip(c), ch
-            two = 0.0 if (topo.mates(a, b) or topo.same_plane(a, b)) else 0.25
-            if (j, core) in P["relayed"]:
-                return 3.0 + two
-            if blocked[c]:
-                return 1.5 + two
-            return (head - on[a].index(c)) % NH + two
-        rem = sorted([c for c in cores if topo.chip(c) != ch], key=lambda c: (when(c), c))
-        peers = sorted([r for r in range(NH) if r != p], key=lambda r: t_q(loc[r]))
-        for i, c in enumerate(rem):
-            order = peers + [p] if i == len(rem) - 1 else [p] + peers
-            units += [(P["rank"][c], r) for r in order]
-    else:
-        pairs = [(c, r) for c in loc for r in range(NH)]
-        pairs.sort(key=lambda cr: (max(t_kv(cr[0]), t_q(loc[cr[1]])), cr[1], cr[0]))
-        units = [(P["rank"][c], r) for c, r in pairs]
     U = len(units)
-    first = {r: min(i for i, u in enumerate(units) if u[1] == r) for r in range(NH)}
-    last = {r: max(i for i, u in enumerate(units) if u[1] == r) for r in range(NH)}
-    fin = sorted(range(NH), key=lambda r: last[r])
+    first, lastu = {}, {}
+    for i, (j, h, r, a) in enumerate(units):
+        first.setdefault(a, i)
+        lastu[a] = i
+    more = {h for _, h, _l in idops}
+    fin = [a for a in sorted(lastu, key=lambda a: lastu[a]) if a not in more] + [h for _, h, l in idops if l]
 
-    te, ve = g.tensor, g.vector
+    def kv_ap(j, h, part):
+        lo = KV * h + KP * part
+        if cores[j] == core:
+            return T.skv[:, lo:lo + KP]
+        return T.kvl[:, j, lo:lo + KP]
+
+    def pt_of(n):
+        return "pp%d" % n, len(P["weng"][pl[n][0]])
+
     seen = set()
 
     def twait(name, n):
@@ -237,56 +295,71 @@ def rank_program(g, core, T, topo):
     for i in range(U + AHEAD):
         if i >= AHEAD:
             u = i - AHEAD
-            j, r = units[u]
+            j, h, r, a = units[u]
+            stop = u == lastu[a] and a not in more
             te.wait_ge(sem.rl, u + 1)
-            mm = te.matmul(T["acc%d" % r][:, 0:QP], T.kvl[:, NH * j + head, KP:2 * KP], T.relu[:, u, :],
-                           u == first[r], u == last[r])
-            if u == last[r]:
+            mm = te.matmul(T["acc%d" % a][:, 0:QP], kv_ap(j, h, 1), T.relu[:, u, :], u == first[a], stop)
+            if stop:
                 mm.then_inc(sem.om, 1)
         if i < U:
-            j, r = units[i]
-            name = "kv%d_%d" % (j, head)
-            twait(name, arr[core, name])
-            if is_rank and r == p:
-                twait("lq%d" % head, 16)
-                qa = T.stage[:, head, 0:QP]
+            j, h, r, a = units[i]
+            if is_rank:
+                if cores[j] == core:
+                    twait("lk%d" % h, 32)
+                else:
+                    twait("kw%d" % j, arr[core, "kw%d" % j])
+                twait("lq%d" % h, 16)
+                qa = T.sq[:, QP * h:QP * h + QP]
             else:
-                twait("q%d" % r, arr[core, "q%d" % r])
-                qa = T.ql[:, r, :]
-            te.matmul(T["s%d" % (i % NB)][:, 0:QP], T.kvl[:, NH * j + head, 0:KP], qa, True, True).then_inc(sem.sm, 1)
+                twait("kv%d_%d" % (j, h), arr[core, "kv%d_%d" % (j, h)])
+                twait("q%d_%d" % (r, h), arr[core, "q%d_%d" % (r, h)])
+                qa = T.ql[:, r, QP * h:QP * h + QP]
+            te.matmul(T["s%d" % (i % NB)][:, 0:QP], kv_ap(j, h, 0), qa, True, True).then_inc(sem.sm, 1)
+    for n, h, l in idops:
+        twait("idn", 1)
+        twait(*pt_of(n))
+        mm = te.matmul(T["acc%d" % h][:, 0:QP], T.ident[:, :], T.part[:, n, :], False, l)
+        if l:
+            mm.then_inc(sem.om, 1)
 
-    ve.memset(T.zero[:, :], 0.0).then_inc(sem.zs, 1)
-    ve.wait_ge(sem.zs, 1)
+    ve.wait_ge(sem.zs, nz)
+    done = [0]
+
+    def evac():
+        a = fin[done[0]]
+        done[0] += 1
+        ve.wait_ge(sem.om, done[0])
+        if not is_rank:
+            ve.tensor_copy(T.obuf[:, a % NH, a // NH, :], T["acc%d" % a][:, 0:QP]).then_inc(sem.ev, 1)
+        elif a in vecp:
+            name, n = pt_of(vecp[a])
+            ve.wait_ge(sem[name], n)
+            ve.tensor_tensor(T.ybuf[:, a, :], T["acc%d" % a][:, 0:QP], T.part[:, vecp[a], :],
+                             AluOpType.add).then_inc(sem.ev, 1)
+        else:
+            ve.tensor_copy(T.ybuf[:, a, :], T["acc%d" % a][:, 0:QP]).then_inc(sem.ev, 1)
+
     for u in range(U):
         ve.wait_ge(sem.sm, u + 1)
         ve.tensor_tensor(T.relu[:, u, :], T["s%d" % (u % NB)][:, 0:QP], T.zero[:, :], AluOpType.max).then_inc(sem.rl, 1)
-    if is_rank:
-        ve.wait_ge(sem.pt, arr_part(topo, helper[ch, head], core))
-    for n, r in enumerate(fin):
-        ve.wait_ge(sem.om, n + 1)
-        if is_rank:
-            ve.tensor_tensor(T.obuf[:, r, :], T["acc%d" % r][:, 0:QP], T.part[:, r, :],
-                             AluOpType.add).then_inc(sem.ev, 1)
-        else:
-            ve.tensor_copy(T.obuf[:, r, :], T["acc%d" % r][:, 0:QP]).then_inc(sem.ev, 1)
+        while not is_rank and done[0] < len(fin) and lastu[fin[done[0]]] + AHEAD <= u:
+            evac()
+    while done[0] < len(fin):
+        evac()
 
     if not is_rank:
-        g.wait_ge(sem.ev, NH)
-        write(T.part[:, :, :], T.obuf[:, :, :], loc[head], "pt")
+        base = min(n for n, x in enumerate(pl) if x[0] == core)
+        for n, a in enumerate(fin):
+            g.wait_ge(sem.ev, n + 1)
+            rid, pid, _ = topo.addr(loc[a % NH])
+            g.remote_dma(T.part[:, base + a // NH, :], T.obuf[:, a % NH, a // NH, :],
+                         sem["pp%d" % (base + a // NH)], sem.ls, pid, rid, _mask(P["weng"][core]))
+            sent[0] += len(P["weng"][core])
         g.wait_ge(sem.ls, sent[0])
         return
-    for n, r in enumerate(fin):
-        if r != p:
-            g.wait_ge(sem.ev, n + 1)
-            write(T.oland[:, head, :], T.obuf[:, r, :], loc[r], "o%d" % head)
-    g.sync.wait_ge(sem.ev, NH)
-    g.sync.dma_start(T.y[:, QP * p:QP * p + QP], T.obuf[:, p, :]).then_inc(sem.st, 16)
-    for qu, h in zip((g.sync, g.scalar), [h for h in range(NH) if h != p]):
-        qu.wait_ge(sem["o%d" % h], len(_bits(topo.mask(loc[h], core))))
-        qu.dma_start(T.y[:, QP * h:QP * h + QP], T.oland[:, h, :]).then_inc(sem.st, 16)
+    for n, h in enumerate(fin):
+        qu = g.sync if n % 2 == 0 else g.scalar
+        qu.wait_ge(sem.ev, n + 1)
+        qu.dma_start(T.y[:, QP * h:QP * h + QP], T.ybuf[:, h, :]).then_inc(sem.st, 16)
     g.wait_ge(sem.ls, sent[0])
     g.wait_ge(sem.st, 16 * NH)
-
-
-def arr_part(topo, src, dst):
-    return len(_bits(topo.mask(src, dst)))

from concourse.bass import DstId, RemoteDMATransfer
from concourse.mybir import AluOpType

NSIM = 32
NH, QP, KP = 3, 256, 128
NR = 9
KV = 2 * KP
NACC = 6
NB = 2
AHEAD = 2

SCRATCH = {
    "skv": ("sbuf", [128, NH * KV], "bfloat16"),
    "sq": ("sbuf", [128, NH * QP], "bfloat16"),
    "kvl": ("sbuf", [128, NR, NH * KV], "bfloat16"),
    "ql": ("sbuf", [128, NH, NH * QP], "bfloat16"),
    "rbuf": ("sbuf", [128, 2, NH * KP], "bfloat16"),
    "zero": ("sbuf", [128, QP], "bfloat16"),
    "ones": ("sbuf", [128, KP], "bfloat16"),
    "ident": ("sbuf", [128, KP], "bfloat16"),
    "relu": ("sbuf", [128, 18, QP], "bfloat16"),
    "obuf": ("sbuf", [128, NH, 2, QP], "bfloat16"),
    "part": ("sbuf", [128, 10, QP], "bfloat16"),
    "ybuf": ("sbuf", [128, NH, QP], "bfloat16"),
}
for _i in range(NACC):
    SCRATCH["acc%d" % _i] = ("psum", [128, 512], "float32")
for _i in range(NB):
    SCRATCH["s%d" % _i] = ("psum", [128, 512], "float32")

SEMAPHORES = (["lk%d" % h for h in range(NH)] + ["lq%d" % h for h in range(NH)]
              + ["kv%d_%d" % (j, h) for j in range(NR) for h in range(NH)]
              + ["kw%d" % j for j in range(NR)]
              + ["q%d_%d" % (r, h) for r in range(NH) for h in range(NH)]
              + ["rh0", "rh1"] + ["pp%d" % n for n in range(10)]
              + ["zs", "idn", "sm", "rl", "om", "ev", "ls", "st"])


def _bits(mask):
    return [e for e in range(32) if (mask >> e) & 1]


def _mask(engs):
    m = 0
    for e in engs:
        m |= 1 << e
    return m


def _split(engs, n):
    w = 1
    while w * 2 * n <= len(engs):
        w *= 2
    return [engs[i * w:(i + 1) * w] for i in range(n)]


def _plan(cores, topo):
    rank = {c: i for i, c in enumerate(cores)}
    allchips = sorted({topo.chip(c) for c in range(NSIM)})
    chips = [ch for ch in allchips if any(topo.chip(c) == ch for c in cores)]
    on = {ch: [c for c in cores if topo.chip(c) == ch] for ch in chips}
    free = {ch: [c for c in range(NSIM) if topo.chip(c) == ch and c not in rank] for ch in allchips}

    def hops(a, b):
        return 0 if a == b else (1 if topo.mates(a, b) or topo.same_plane(a, b) else 2)

    late = {ch: [s for s in cores if topo.chip(s) != ch and not all(topo.may_write(s, d) for d in on[ch])]
            for ch in chips}
    blocked = {s: any(s in late[ch] for ch in chips) for s in cores}

    def when(s, ch, h):
        a = topo.chip(s)
        return (h - on[a].index(s)) % NH + (2.0 if blocked[s] else 0.0) + 0.25 * hops(a, ch)

    work = {c: [] for ch in chips for c in free[ch]}
    keys, dest, pairs = {}, {}, {}
    for ch in chips:
        loc = on[ch]
        nl, nf = len(loc), len(free[ch])
        pcs = []
        for h in range(NH):
            lst = [(when(s, ch, h), s, h) for s in cores if topo.chip(s) != ch and s not in late[ch]]
            pcs += sorted(lst, key=lambda x: (x[0], x[1]))
        for n, (_, s, h) in enumerate(pcs):
            w = free[ch][min(nf - 1, int((n + 0.5) * nf / len(pcs)))]
            dest[ch, s, h] = w
            work[w] += [(rank[s], h, r) for r in range(nl)]
        pairs[ch] = []
        for w in free[ch]:
            hq = []
            for _, h, _r in work[w]:
                if h not in hq:
                    hq.append(h)
            if len(hq) == 2:
                grp = [[u for u in work[w] if u[1] == h] for h in hq[::-1]]
            else:
                grp = [[u for u in work[w] if u[:2] == work[w][0][:2]], [u for u in work[w] if u[:2] != work[w][0][:2]]]
            grp = [x for x in grp if x]
            pairs[ch] += [(w, x[0][1], i) for i, x in enumerate(grp)]
            work[w] = [u + (i * NH + u[2],) for i, x in enumerate(grp) for u in x]
        for p, c in enumerate(loc):
            keys[c] = ([c] + [loc[(p + i) % nl] for i in range(1, nl)]
                       + sorted(late[ch], key=lambda s: (hops(topo.chip(s), ch), s)))

    relay = {}
    for s in cores:
        ch = topo.chip(s)
        for c in chips:
            if s not in late[c]:
                continue
            mid = []
            if hops(ch, c) == 2:
                mid = [x for x in allchips if x not in on and hops(ch, x) == 1 and hops(x, c) == 1]
            two = []
            for xc in mid + [ch]:
                rel = [x for x in free[xc] if topo.may_write(s, x) and all(topo.may_write(x, d) for d in on[c])]
                byd = {}
                for x in rel:
                    byd.setdefault(topo.die(x), x)
                two = sorted(byd.values())[:2] if len(byd) >= 2 else rel[:2]
                if len(two) == 2:
                    break
            relay[s, c] = two
    weng = {w: _bits(topo.mask(w, on[[c for c in chips if c != ch][0]][0])) for ch in chips for w in free[ch]}

    calls = {c: [] for c in range(NSIM)}
    arr, fwd, nslot = {}, {}, {}

    def add(core, waits, trs):
        for t in trs:
            for d in t["dsts"]:
                arr[d, t["sem"]] = arr.get((d, t["sem"]), 0) + len(t["engs"])
        calls[core].append((waits, trs))

    for j, s in enumerate(cores):
        ch = topo.chip(s)
        p = on[ch].index(s)
        far = [c for c in chips if c != ch]
        eall = _bits(topo.mask(s, free[ch][0]))
        eoff = _bits(topo.mask(s, on[far[0]][0]))
        eon = [e for e in eall if e not in eoff]
        hs = [(p + i) % NH for i in range(NH)]

        def deal(offs, ons):
            for t, e in zip(offs, _split(eoff, max(1, len(offs)))):
                t["engs"] = e
            for t, e in zip(ons, _split(eon if offs else eall, max(1, len(ons)))):
                t["engs"] = e
            return offs + ons

        offs, ons = [], []
        half = NH * KP
        for c in far:
            if s not in late[c]:
                continue
            for i, x in enumerate(relay[s, c]):
                slot = nslot.get(x, 0)
                nslot[x] = slot + 1
                t = {"src": ("skv", i * half, (i + 1) * half), "dst": ("rb", slot), "dsts": [x], "sem": "rh%d" % slot}
                (ons if topo.chip(x) == ch else offs).append(t)
                fwd.setdefault(x, []).append((j, i * half, (i + 1) * half, slot, list(on[c])))
        whole = [{"src": ("skv", 0, NH * KV), "dst": ("kvl", j, 0, NH * KV), "dsts": [c for c in on[ch] if c != s],
                  "sem": "kw%d" % j}]
        if blocked[s]:
            add(s, [("lk%d" % h, 32) for h in hs], deal(offs, ons))
            add(s, [], deal([], whole))
        for h in hs:
            lo = KV * h
            offs = [{"src": ("skv", lo, lo + KV), "dst": ("kvl", j, lo, lo + KV), "dsts": [dest[c, s, h]],
                     "sem": "kv%d_%d" % (j, h)} for c in far if s not in late[c]]
            qd = [w for w in free[ch] if any(u[1] == h for u in work[w])]
            ons = [{"src": ("sq", h), "dst": ("ql", p, h), "dsts": qd, "sem": "q%d_%d" % (p, h)}]
            add(s, [("lk%d" % h, 32), ("lq%d" % h, 16)], deal(offs, ons))
        if not blocked[s]:
            add(s, [], deal([], whole))
    for x, lst in fwd.items():
        for j, lo, hi, slot, dsts in lst:
            add(x, [("rh%d" % slot, None)],
                [{"src": ("rb", slot), "dst": ("kvl", j, lo, hi), "dsts": dsts, "sem": "kw%d" % j,
                  "engs": _bits(topo.mask(x, dsts[0]))}])
    return {"rank": rank, "on": on, "free": free, "calls": calls, "arr": arr, "blocked": blocked,
            "work": work, "keys": keys, "pairs": pairs, "weng": weng}


def rank_program(g, core, T, topo):
    cores = list(T.cores)
    P = _plan(cores, topo)
    on, arr, work = P["on"], P["arr"], P["work"]
    ch = topo.chip(core)
    is_rank = core in P["rank"]
    mine = work.get(core, [])
    if not is_rank and not mine and not P["calls"][core]:
        return
    sem = T.sem
    sent = [0]
    te, ve = g.tensor, g.vector

    def ap(spec):
        kind = spec[0]
        if kind == "skv":
            return T.skv[:, spec[1]:spec[2]]
        if kind == "sq":
            return T.sq[:, QP * spec[1]:QP * spec[1] + QP]
        if kind == "kvl":
            return T.kvl[:, spec[1], spec[2]:spec[3]]
        if kind == "ql":
            return T.ql[:, spec[1], QP * spec[2]:QP * spec[2] + QP]
        return T.rbuf[:, spec[1], :]

    def dst_id(d):
        rid, pid, _ = topo.addr(d)
        return DstId(rid=rid, pnc=pid)

    idops, vecp = [], {}
    units = []
    if is_rank:
        loc = on[ch]
        pl = P["pairs"][ch]
        p = loc.index(core)
        hs = [(p + i) % NH for i in range(NH)]
        for c in P["keys"][core]:
            units += [(P["rank"][c], h, p, h) for h in (hs if c == core else range(NH))]
        for h in range(NH):
            ph = sorted((i, n) for n, (w, hh, i) in enumerate(pl) if hh == h)
            if ph:
                vecp[h] = ph[-1][1]
            idops += [(i, n, h, (i, n) == ph[-2]) for i, n in ph[:-1]]
        idops = [x[1:] for x in sorted(idops)]
    elif mine:
        loc = on[ch]
        pl = P["pairs"][ch]
        units = list(mine)

    if is_rank:
        if P["blocked"][core]:
            items = [(w, h) for h in hs for w in "kv"] + [("q", h) for h in hs]
        else:
            items = [(w, h) for h in hs for w in "kvq"]
        for i, (w, h) in enumerate(items):
            qu = g.sync if i % 2 == 0 else g.scalar
            if w == "k":
                qu.dma_start(T.skv[:, KV * h:KV * h + KP], T.k[:, KP * h:KP * h + KP]).then_inc(sem["lk%d" % h], 16)
            elif w == "v":
                qu.dma_start(T.skv[:, KV * h + KP:KV * h + KV],
                             T.v[:, KP * h:KP * h + KP]).then_inc(sem["lk%d" % h], 16)
            else:
                qu.dma_start(T.sq[:, QP * h:QP * h + QP], T.q[:, QP * h:QP * h + QP]).then_inc(sem["lq%d" % h], 16)

    nz = 0
    if units:
        ve.memset(T.zero[:, :], 0.0).then_inc(sem.zs, 1)
        nz = 1
        if idops:
            ve.memset(T.ones[:, :], 1.0).then_inc(sem.zs, 1)
            nz = 2
            g.wait_ge(sem.zs, nz)
            g.affine_select(T.ident[:, :], T.ones[:, :], [[-1, KP]], AluOpType.is_equal, 0.0, 0, 1).then_inc(sem.idn, 1)

    for waits, trs in P["calls"][core]:
        for name, n in waits:
            g.wait_ge(sem[name], arr[core, name] if n is None else n)
        g.remote_dma_fused(
            [RemoteDMATransfer(dst_ids=[dst_id(d) for d in t["dsts"]], dma_engine_mask=_mask(t["engs"]),
                               remote_sem=sem[t["sem"]], srcs=[ap(t["src"])], dsts=[ap(t["dst"]) for _ in t["dsts"]],
                               alu_op=0) for t in trs], local_sem=sem.ls)
        sent[0] += sum(len(t["engs"]) for t in trs)
    if not units:
        g.wait_ge(sem.ls, sent[0])
        return

    U = len(units)
    first, lastu = {}, {}
    for i, (j, h, r, a) in enumerate(units):
        first.setdefault(a, i)
        lastu[a] = i
    more = {h for _, h, _l in idops}
    fin = [a for a in sorted(lastu, key=lambda a: lastu[a]) if a not in more] + [h for _, h, l in idops if l]

    def kv_ap(j, h, part):
        lo = KV * h + KP * part
        if cores[j] == core:
            return T.skv[:, lo:lo + KP]
        return T.kvl[:, j, lo:lo + KP]

    def pt_of(n):
        return "pp%d" % n, len(P["weng"][pl[n][0]])

    seen = set()

    def twait(name, n):
        if name not in seen:
            seen.add(name)
            te.wait_ge(sem[name], n)

    for i in range(U + AHEAD):
        if i >= AHEAD:
            u = i - AHEAD
            j, h, r, a = units[u]
            stop = u == lastu[a] and a not in more
            te.wait_ge(sem.rl, u + 1)
            mm = te.matmul(T["acc%d" % a][:, 0:QP], kv_ap(j, h, 1), T.relu[:, u, :], u == first[a], stop)
            if stop:
                mm.then_inc(sem.om, 1)
        if i < U:
            j, h, r, a = units[i]
            if is_rank:
                if cores[j] == core:
                    twait("lk%d" % h, 32)
                else:
                    twait("kw%d" % j, arr[core, "kw%d" % j])
                twait("lq%d" % h, 16)
                qa = T.sq[:, QP * h:QP * h + QP]
            else:
                twait("kv%d_%d" % (j, h), arr[core, "kv%d_%d" % (j, h)])
                twait("q%d_%d" % (r, h), arr[core, "q%d_%d" % (r, h)])
                qa = T.ql[:, r, QP * h:QP * h + QP]
            te.matmul(T["s%d" % (i % NB)][:, 0:QP], kv_ap(j, h, 0), qa, True, True).then_inc(sem.sm, 1)
    for n, h, l in idops:
        twait("idn", 1)
        twait(*pt_of(n))
        mm = te.matmul(T["acc%d" % h][:, 0:QP], T.ident[:, :], T.part[:, n, :], False, l)
        if l:
            mm.then_inc(sem.om, 1)

    ve.wait_ge(sem.zs, nz)
    done = [0]

    def evac():
        a = fin[done[0]]
        done[0] += 1
        ve.wait_ge(sem.om, done[0])
        if not is_rank:
            ve.tensor_copy(T.obuf[:, a % NH, a // NH, :], T["acc%d" % a][:, 0:QP]).then_inc(sem.ev, 1)
        elif a in vecp:
            name, n = pt_of(vecp[a])
            ve.wait_ge(sem[name], n)
            ve.tensor_tensor(T.ybuf[:, a, :], T["acc%d" % a][:, 0:QP], T.part[:, vecp[a], :],
                             AluOpType.add).then_inc(sem.ev, 1)
        else:
            ve.tensor_copy(T.ybuf[:, a, :], T["acc%d" % a][:, 0:QP]).then_inc(sem.ev, 1)

    for u in range(U):
        ve.wait_ge(sem.sm, u + 1)
        ve.tensor_tensor(T.relu[:, u, :], T["s%d" % (u % NB)][:, 0:QP], T.zero[:, :], AluOpType.max).then_inc(sem.rl, 1)
        while not is_rank and done[0] < len(fin) and lastu[fin[done[0]]] + AHEAD <= u:
            evac()
    while done[0] < len(fin):
        evac()

    if not is_rank:
        base = min(n for n, x in enumerate(pl) if x[0] == core)
        for n, a in enumerate(fin):
            g.wait_ge(sem.ev, n + 1)
            rid, pid, _ = topo.addr(loc[a % NH])
            g.remote_dma(T.part[:, base + a // NH, :], T.obuf[:, a % NH, a // NH, :],
                         sem["pp%d" % (base + a // NH)], sem.ls, pid, rid, _mask(P["weng"][core]))
            sent[0] += len(P["weng"][core])
        g.wait_ge(sem.ls, sent[0])
        return
    for n, h in enumerate(fin):
        qu = g.sync if n % 2 == 0 else g.scalar
        qu.wait_ge(sem.ev, n + 1)
        qu.dma_start(T.y[:, QP * h:QP * h + QP], T.ybuf[:, h, :]).then_inc(sem.st, 16)
    g.wait_ge(sem.ls, sent[0])
    g.wait_ge(sem.st, 16 * NH)
